import numpy as np
import ml_dtypes


def mxq(x, axis, fmt="e4m3"):
    dtype, down = {"e4m3": (ml_dtypes.float8_e4m3fn, 7), "e5m2": (ml_dtypes.float8_e5m2, 14)}[fmt]
    v = np.moveaxis(np.asarray(x, np.float32).astype(ml_dtypes.bfloat16).astype(np.float64), axis, -1)
    blocks = v.reshape(v.shape[:-1] + (-1, 32))
    amax = np.abs(blocks).max(-1, keepdims=True)
    byte = np.maximum(np.where(amax > 0, np.frexp(amax)[1] - 1 + 127, 0) - down, 1)
    scale = np.exp2(byte - 127.0)
    codes = (blocks / scale).astype(np.float32).astype(dtype).astype(np.float64)
    return np.moveaxis((codes * scale).reshape(v.shape), -1, axis)


WIDE = False


def mx_kscale(k):
    if not WIDE:
        return np.ones(k)
    levels = np.array([10, -10, 5, -5, 0])
    if k % 512:
        return np.exp2(np.random.permutation(np.resize(levels, k // 32))).repeat(32)
    a = np.empty((k // 512, 16))
    for p in range(k // 512):
        a[p, :8] = np.random.permutation(np.resize(levels, 8))
        for g in range(8):
            far = levels[np.abs(levels - a[p, g]) >= 10]
            a[p, g + 8] = far[np.random.randint(len(far))]
    return np.exp2(a.ravel()).repeat(32)


def f64(x):
    return np.asarray(x).astype(np.float64)


def striped(idx):
    return np.tile(idx.reshape(-1, 16).T, (8, 1)).astype(np.uint16)


def unstriped(offs):
    return offs[:16].T.reshape(-1).astype(np.int64)


def pack_weight(w):
    k, n = w.shape
    w = f64(np.asarray(w, np.float32).astype(ml_dtypes.bfloat16)).reshape(k // 32, 32, n)
    amax = np.abs(w).max(1)
    byte = np.clip(np.where(amax > 0, np.frexp(amax)[1] - 1 + 127 - 7, 1), 1, 254)
    scaled = (w * np.exp2(127.0 - byte)[:, None, :]).reshape(k, n).astype(np.float32)
    words = np.ascontiguousarray(scaled.reshape(k // 512, 128, 4, n).transpose(0, 1, 3, 2)).astype(ml_dtypes.float8_e4m3fn).view(np.uint8)
    return words, np.ascontiguousarray(byte.astype(np.uint8).reshape(k // 512, 16, n))


def unpack_weight(words, scales):
    g, p, n, _ = words.shape
    vals = np.ascontiguousarray(words).view(ml_dtypes.float8_e4m3fn).astype(np.float64) * np.repeat(np.exp2(scales.astype(np.float64) - 127.0), 8, axis=1)[..., None]
    return vals.transpose(0, 1, 3, 2).reshape(g * 512, n)


E2M1 = np.array([0.0, 0.5, 1.0, 1.5, 2.0, 3.0, 4.0, 6.0, -0.0, -0.5, -1.0, -1.5, -2.0, -3.0, -4.0, -6.0])


def pack_fp4(w):
    k, n = w.shape
    w = f64(np.asarray(w, np.float32).astype(ml_dtypes.bfloat16)).reshape(k // 32, 32, n)
    amax = np.abs(w).max(1)
    mant, ex = np.frexp(amax / 6.0)
    byte = np.clip(np.where(amax > 0, np.where(mant > 0.5, ex, ex - 1) + 127, 1), 1, 254)
    scaled = (w * np.exp2(127.0 - byte)[:, None, :]).reshape(k, n).astype(np.float32)
    c = np.ascontiguousarray(scaled.reshape(k // 512, 128, 4, n).transpose(0, 1, 3, 2)).astype(ml_dtypes.float4_e2m1fn).view(np.uint8) & 0xF
    words = (c[..., 0::2] | (c[..., 1::2] << 4)).reshape(k // 512, 128, 2 * n)
    return np.ascontiguousarray(words), np.ascontiguousarray(byte.astype(np.uint8).reshape(k // 512, 16, n))


def unpack_fp4(words, scales):
    g, _, n = scales.shape
    words = np.ascontiguousarray(words).reshape(g, 128, n, 2)
    nib = np.empty((g, 128, n, 4), np.uint8)
    nib[..., 0::2] = words & 0xF
    nib[..., 1::2] = words >> 4
    vals = E2M1[nib] * np.repeat(np.exp2(scales.astype(np.float64) - 127.0), 8, axis=1)[..., None]
    return vals.transpose(0, 1, 3, 2).reshape(g * 512, n)


K, T, S, N, H = 1024, 2048, 512, 128, 512


def setup_inputs():
    n = np.random.standard_normal
    s = mx_kscale(K)[:, None]
    u = mx_kscale(H)
    packed_xT = pack_weight(n((K, T)) * s)
    packed_w1 = pack_fp4(n((K, H)) / np.sqrt(K) / s)
    packed_w2 = pack_fp4(n((K, H)) / np.sqrt(K) / s)
    packed_w3 = pack_fp4(n((H, N)) / np.sqrt(H) / u[:, None])
    return {
        "x_words": packed_xT[0],
        "x_scales": packed_xT[1],
        "w1_words": packed_w1[0],
        "w1_scales": packed_w1[1],
        "w2_words": packed_w2[0],
        "w2_scales": packed_w2[1],
        "bx": (np.random.uniform(0.3, 0.9, (H, 1))).astype(np.float32),
        "gx": (np.random.uniform(0.3, 0.9, (H, 1))).astype(np.float32),
        "unit": (np.random.uniform(0.6, 1.4, (H, 1)) * u[:, None]).astype(np.float32),
        "w3_words": packed_w3[0],
        "w3_scales": packed_w3[1],
        "offs": striped(np.random.permutation(T)[:S]),
        "prv": striped(np.random.permutation(S)),
        "coh": striped(np.random.permutation(S)),
    }


def reference(x_words, x_scales, w1_words, w1_scales, w2_words, w2_scales, bx, gx, unit, w3_words, w3_scales, offs, prv, coh):
    xq = unpack_weight(x_words, x_scales)[:, unstriped(offs)]
    kt = unpack_fp4(w1_words, w1_scales).T @ xq
    ya = unpack_fp4(w2_words, w2_scales).T @ xq
    gc = ya[:, unstriped(coh)]
    lm = f64(bx) * kt + f64(gx) * gc
    mx = np.exp(1.2 * np.tanh(lm))
    qx = -1.0 * np.exp(-1.0 * mx) + 1.0
    kp = kt[:, unstriped(prv)]
    dk = kt - kp
    hid = f64(unit) * (np.log(qx + 0.05) + dk)
    return unpack_fp4(w3_words, w3_scales).T @ mxq(hid, 0, "e4m3")

@@ -1,0 +1,190 @@
+from contextlib import ExitStack
+
+import concourse.mybir as mybir
+
+K, T, S, N, H = 1024, 2048, 512, 128, 512
+FLOPS = 2 * (2 * K * H * S + H * N * S)
+
+F32 = mybir.dt.float32
+BF16 = mybir.dt.bfloat16
+I32 = mybir.dt.int32
+U32 = mybir.dt.uint32
+U16 = mybir.dt.uint16
+U8 = mybir.dt.uint8
+FP8X4 = mybir.dt.float8_e4m3fn_x4
+FP4X4 = mybir.dt.float4_e2m1fn_x4
+ACT = mybir.ActivationFunctionType
+ALU = mybir.AluOpType
+
+P = 128
+PACK = 4
+PASSES = K // (P * PACK)
+QUADS = 4
+HALF = S // 2
+ROW0 = P - 16
+PIECES = ((0, 256), (256, 128), (384, 128))
+
+
+def tile_picked_yleeca_log_p_kernel(
+    tc, x_words, x_scales, w1_words, w1_scales, w2_words, w2_scales, bx, gx, unit, w3_words, w3_scales, offs, prv, coh, out
+):
+    nc = tc.nc
+    with ExitStack() as ctx:
+        keep = ctx.enter_context(tc.tile_pool(name="keep", bufs=1))
+        psum = ctx.enter_context(tc.psum_pool(name="psum", bufs=1))
+
+        def load_scale_rows(queue, plane, scales):
+            for q in range(QUADS):
+                queue.dma_start(
+                    out=plane[32 * q : 32 * q + 4, :, :].bitcast(I32),
+                    in_=scales[:, 4 * q : 4 * q + 4, :].rearrange("o r c -> r o c").bitcast(I32),
+                )
+
+        offs_t = keep.tile([P, S // 16], U16, name="offs_t")
+        coh_t = keep.tile([P, S // 16], U16, name="coh_t")
+        prv_t = keep.tile([P, S // 16], U16, name="prv_t")
+        xs_all = keep.tile([P, PASSES, T], U8, name="xs_all", tag="second", align_bytes=64)
+        xs = keep.tile([P, PASSES, S], U8, name="xs", align_bytes=64)
+        w2s_raw = keep.tile([P, PASSES, H], U8, name="w2s_raw", align_bytes=64)
+        w1s_raw = keep.tile([P, PASSES, H], U8, name="w1s_raw", align_bytes=64)
+        nc.vector.memset(w2s_raw[:].bitcast(I32), 0)
+        nc.vector.memset(w1s_raw[:].bitcast(I32), 0)
+        nc.vector.memset(xs_all[0:ROW0, :, :].bitcast(I32), 0)
+        nc.vector.memset(xs[:].bitcast(I32), 0)
+
+        nc.sync.dma_start(offs_t[:], offs)
+        nc.scalar.dma_start(out=xs_all[ROW0:P, :, :].bitcast(I32), in_=x_scales.rearrange("o q c -> q o c").bitcast(I32))
+        nc.sync.dma_start(coh_t[:], coh)
+        nc.sync.dma_start(prv_t[:], prv)
+
+        xw_first = keep.tile([P, T], U32, name="xw_first", align_bytes=64)
+        w2w_raw = keep.tile([P, PASSES, 2 * H], U8, name="w2w_raw", align_bytes=64)
+        w1w_raw = keep.tile([P, PASSES, 2 * H], U8, name="w1w_raw", align_bytes=64)
+        nc.sync.dma_start(out=xw_first[:].bitcast(I32), in_=x_words[0].rearrange("p n t -> p (n t)").bitcast(I32))
+        nc.sync.dma_start(out=w2w_raw[:].bitcast(I32), in_=w2_words.rearrange("o p c -> p o c").bitcast(I32))
+        nc.sync.dma_start(out=w1w_raw[:].bitcast(I32), in_=w1_words.rearrange("o p c -> p o c").bitcast(I32))
+
+        gx_t = keep.tile([P, PACK], F32, name="gx_t")
+        bx_t = keep.tile([P, PACK], F32, name="bx_t")
+        unit_t = keep.tile([P, PACK], F32, name="unit_t")
+        nc.gpsimd.dma_start(out=gx_t[:], in_=gx.rearrange("(p t) one -> p (t one)", t=PACK))
+        nc.gpsimd.dma_start(out=unit_t[:], in_=unit.rearrange("(p t) one -> p (t one)", t=PACK))
+        nc.gpsimd.dma_start(out=bx_t[:], in_=bx.rearrange("(p t) one -> p (t one)", t=PACK))
+        load_scale_rows(nc.scalar, w2s_raw, w2_scales)
+        load_scale_rows(nc.sync, w1s_raw, w1_scales)
+
+        xs_picked = keep.tile([P, PASSES, S], U8, name="xs_picked", align_bytes=64)
+        xw = [keep.tile([P, S], U32, name="xw%d" % o, align_bytes=64) for o in range(PASSES)]
+        w2s = keep.tile([P, PASSES, H], U8, name="w2s", align_bytes=64)
+        w1s = keep.tile([P, PASSES, H], U8, name="w1s", align_bytes=64)
+        w2w = keep.tile([P, PASSES, 2 * H], U8, name="w2w", align_bytes=64)
+        w1w = keep.tile([P, PASSES, 2 * H], U8, name="w1w", align_bytes=64)
+
+        def deal_scales(dealt, raw):
+            nc.vector.tensor_copy(
+                out=dealt[:].rearrange("p o (t m) -> p o t m", t=PACK),
+                in_=raw[:].rearrange("p o (m t) -> p o t m", t=PACK),
+            )
+
+        def deal_words(dealt, raw):
+            nc.scalar.copy(
+                out=dealt[:].bitcast(U16).rearrange("p o (t m) -> p o t m", t=PACK),
+                in_=raw[:].bitcast(U16).rearrange("p o (m t) -> p o t m", t=PACK),
+            )
+
+        for o in range(PASSES):
+            nc.vector.tensor_copy(xs_picked[:, o, :], xs_all[:, o, :].indirect(offs_t[:]))
+        xw_second = keep.tile([P, T], U32, name="xw_second", tag="second", align_bytes=64)
+        nc.scalar.dma_start(out=xw_second[:].bitcast(I32), in_=x_words[1].rearrange("p n t -> p (n t)").bitcast(I32))
+        for q in range(QUADS):
+            nc.sync.dma_start(
+                out=xs[32 * q : 32 * q + 4, :, :].bitcast(I32), in_=xs_picked[ROW0 + 4 * q : ROW0 + 4 * q + 4, :, :].bitcast(I32)
+            )
+        nc.vector.tensor_copy(xw[0][:], xw_first[:].indirect(offs_t[:]))
+        deal_words(w2w, w2w_raw)
+        deal_words(w1w, w1w_raw)
+        deal_scales(w2s, w2s_raw)
+        deal_scales(w1s, w1s_raw)
+        nc.vector.tensor_copy(xw[1][:], xw_second[:].indirect(offs_t[:]))
+
+        nc.sync.dma_start(out=w2w_raw[:, 0, 0 : 2 * N].bitcast(I32), in_=w3_words[0].bitcast(I32))
+        load_scale_rows(nc.sync, w2s_raw[:, 0:1, 0:N], w3_scales)
+
+        ya_ps = [psum.tile([P, S], F32, name="ya_ps%d" % t, tag="ya%d" % t) for t in range(PACK)]
+        kt_ps = [psum.tile([P, S], F32, name="kt_ps%d" % t, tag="kt%d" % t) for t in range(PACK)]
+
+        def product(acc, words, scales, t, o):
+            nc.tensor.matmul_mx(
+                out=acc[:],
+                lhsT=words[:, o, 2 * P * t : 2 * P * (t + 1)].bitcast(FP4X4),
+                lhsT_scale=scales[:, o, P * t : P * (t + 1)],
+                rhs=xw[o][:].bitcast(FP8X4),
+                rhs_scale=xs[:, o, :],
+                start=(o == 0),
+                stop=(o == PASSES - 1),
+            )
+
+        for o in range(PASSES):
+            for t in range(PACK):
+                product(ya_ps[t], w2w, w2s, t, o)
+                product(kt_ps[t], w1w, w1s, t, o)
+
+        cohort = [keep.tile([P, S], F32, name="cohort%d" % t) for t in range(PACK)]
+        period = [keep.tile([P, S], F32, name="period%d" % t) for t in range(PACK)]
+        fetched = [keep.tile([P, S], F32, name="fetched%d" % t) for t in range(PACK)]
+        earlier = [keep.tile([P, S], F32, name="earlier%d" % t) for t in range(PACK)]
+        lm = [keep.tile([P, S], F32, name="lm%d" % t) for t in range(PACK)]
+        th = [keep.tile([P, S], F32, name="th%d" % t) for t in range(PACK)]
+        mx = [keep.tile([P, S], F32, name="mx%d" % t) for t in range(PACK)]
+        change = [keep.tile([P, S], F32, name="change%d" % t) for t in range(PACK)]
+        alive = keep.tile([P, PACK, S], F32, name="alive")
+        logq = keep.tile([P, PACK, S], F32, name="logq")
+
+        def fetch(dst, window, lst):
+            for c0 in range(0, S, HALF):
+                nc.vector.tensor_copy(dst[:, c0 : c0 + HALF], window[:].indirect(lst[:, c0 // 16 : (c0 + HALF) // 16]))
+
+        for t in range(PACK):
+            nc.scalar.activation(out=cohort[t][:], in_=ya_ps[t][:], func=ACT.Copy, scale=gx_t[:, t : t + 1])
+            nc.scalar.activation(out=period[t][:], in_=kt_ps[t][:], func=ACT.Copy, scale=unit_t[:, t : t + 1])
+        for t in range(PACK):
+            fetch(fetched[t], cohort[t], coh_t)
+            nc.vector.scalar_tensor_tensor(
+                out=lm[t][:], in0=kt_ps[t][:], scalar=bx_t[:, t : t + 1], in1=fetched[t][:], op0=ALU.mult, op1=ALU.add
+            )
+        for t in range(PACK):
+            nc.scalar.activation(out=th[t][:], in_=lm[t][:], func=ACT.Tanh)
+            nc.scalar.activation(out=mx[t][:], in_=th[t][:], func=ACT.Exp, scale=1.2)
+            nc.scalar.activation(out=alive[:, t, :], in_=mx[t][:], func=ACT.Exp, scale=-1.0)
+        for t in range(PACK):
+            fetch(earlier[t], period[t], prv_t)
+            nc.vector.scalar_tensor_tensor(
+                out=change[t][:], in0=kt_ps[t][:], scalar=unit_t[:, t : t + 1], in1=earlier[t][:], op0=ALU.mult, op1=ALU.subtract
+            )
+
+        for i, (c0, n) in enumerate(PIECES):
+            cols = slice(c0, c0 + n)
+            nc.scalar.activation(out=logq[:, :, cols], in_=alive[:, :, cols], func=ACT.Ln, scale=-1.0, bias=1.05)
+            hid = keep.tile([P, PACK, n], BF16, name="hid%d" % i, align_bytes=64)
+            for t in range(PACK):
+                nc.vector.scalar_tensor_tensor(
+                    out=hid[:, t, :], in0=logq[:, t, cols], scalar=unit_t[:, t : t + 1], in1=change[t][:, cols], op0=ALU.mult, op1=ALU.add
+                )
+            woven = keep.tile([P, n, PACK], BF16, name="woven%d" % i, align_bytes=64)
+            nc.vector.tensor_copy(out=woven[:], in_=hid[:].rearrange("p t n -> p n t"))
+            codes = keep.tile([P, n], U32, name="codes%d" % i, align_bytes=64)
+            plane = keep.tile([P, n], U8, name="plane%d" % i, align_bytes=64)
+            nc.vector.quantize_mx(out=codes[:].bitcast(FP8X4), scales=plane[:], in_=woven[:].rearrange("p n t -> p (n t)"))
+            acc = psum.tile([P, n], F32, name="out_ps%d" % i, tag="ya%d" % i)
+            nc.tensor.matmul_mx(
+                out=acc[:],
+                lhsT=w2w_raw[:, 0, 0 : 2 * N].bitcast(FP4X4),
+                lhsT_scale=w2s_raw[:, 0, 0:N],
+                rhs=codes[:].bitcast(FP8X4),
+                rhs_scale=plane[:],
+                start=True,
+                stop=True,
+            )
+            res = keep.tile([P, n], F32, name="res%d" % i)
+            nc.scalar.copy(out=res[:], in_=acc[:])
+            nc.sync.dma_start(out=out[:, cols], in_=res[:])

@@ -20,8 +20,9 @@ P = 128
 PACK = 4
 PASSES = K // (P * PACK)
 QUADS = 4
-HALF = S // 2
+SPARE = 192
 ROW0 = P - 16
+ON_VECTOR = 1
 PIECES = ((0, 256), (256, 128), (384, 128))
 
 
@@ -43,38 +44,44 @@ def tile_picked_yleeca_log_p_kernel(
         offs_t = keep.tile([P, S // 16], U16, name="offs_t")
         coh_t = keep.tile([P, S // 16], U16, name="coh_t")
         prv_t = keep.tile([P, S // 16], U16, name="prv_t")
-        xs_all = keep.tile([P, PASSES, T], U8, name="xs_all", tag="second", align_bytes=64)
+        xs_all = keep.tile([P, PASSES, T], U8, name="xs_all", tag="after_xs", align_bytes=64)
         xs = keep.tile([P, PASSES, S], U8, name="xs", align_bytes=64)
-        w2s_raw = keep.tile([P, PASSES, H], U8, name="w2s_raw", align_bytes=64)
-        w1s_raw = keep.tile([P, PASSES, H], U8, name="w1s_raw", align_bytes=64)
+        w2s_raw = keep.tile([P, PASSES, H], U8, name="w2s_raw", tag="after_w2s", align_bytes=64)
         nc.vector.memset(w2s_raw[:].bitcast(I32), 0)
-        nc.vector.memset(w1s_raw[:].bitcast(I32), 0)
         nc.vector.memset(xs_all[0:ROW0, :, :].bitcast(I32), 0)
         nc.vector.memset(xs[:].bitcast(I32), 0)
+        cohort = keep.tile([P, PACK * S + SPARE], F32, name="cohort")
+        period = keep.tile([P, PACK * S + SPARE], F32, name="period")
+        nc.vector.memset(cohort[:, PACK * S :], 0.0)
+        nc.vector.memset(period[:, PACK * S :], 0.0)
+
+        def rows(tile, t, width=S):
+            c0 = (PACK - 1 - t) * S
+            return tile[:, c0 : c0 + width]
 
         nc.sync.dma_start(offs_t[:], offs)
         nc.scalar.dma_start(out=xs_all[ROW0:P, :, :].bitcast(I32), in_=x_scales.rearrange("o q c -> q o c").bitcast(I32))
-        nc.sync.dma_start(coh_t[:], coh)
-        nc.sync.dma_start(prv_t[:], prv)
 
         xw_first = keep.tile([P, T], U32, name="xw_first", align_bytes=64)
+        xw_second = keep.tile([P, T], U32, name="xw_second", align_bytes=64)
         w2w_raw = keep.tile([P, PASSES, 2 * H], U8, name="w2w_raw", align_bytes=64)
         w1w_raw = keep.tile([P, PASSES, 2 * H], U8, name="w1w_raw", align_bytes=64)
-        nc.sync.dma_start(out=xw_first[:].bitcast(I32), in_=x_words[0].rearrange("p n t -> p (n t)").bitcast(I32))
-        nc.sync.dma_start(out=w2w_raw[:].bitcast(I32), in_=w2_words.rearrange("o p c -> p o c").bitcast(I32))
-        nc.sync.dma_start(out=w1w_raw[:].bitcast(I32), in_=w1_words.rearrange("o p c -> p o c").bitcast(I32))
-
         gx_t = keep.tile([P, PACK], F32, name="gx_t")
         bx_t = keep.tile([P, PACK], F32, name="bx_t")
         unit_t = keep.tile([P, PACK], F32, name="unit_t")
-        nc.gpsimd.dma_start(out=gx_t[:], in_=gx.rearrange("(p t) one -> p (t one)", t=PACK))
+        nc.sync.dma_start(out=xw_first[:].bitcast(I32), in_=x_words[0].rearrange("p n t -> p (n t)").bitcast(I32))
+        nc.sync.dma_start(coh_t[:], coh)
+        nc.sync.dma_start(prv_t[:], prv)
+        nc.sync.dma_start(out=gx_t[:], in_=gx.rearrange("(p t) one -> p (t one)", t=PACK))
+        nc.gpsimd.dma_start(out=w2w_raw[:].bitcast(I32), in_=w2_words.rearrange("o p c -> p o c").bitcast(I32))
+        nc.gpsimd.dma_start(out=xw_second[:].bitcast(I32), in_=x_words[1].rearrange("p n t -> p (n t)").bitcast(I32))
+        nc.gpsimd.dma_start(out=w1w_raw[:].bitcast(I32), in_=w1_words.rearrange("o p c -> p o c").bitcast(I32))
         nc.gpsimd.dma_start(out=unit_t[:], in_=unit.rearrange("(p t) one -> p (t one)", t=PACK))
         nc.gpsimd.dma_start(out=bx_t[:], in_=bx.rearrange("(p t) one -> p (t one)", t=PACK))
         load_scale_rows(nc.scalar, w2s_raw, w2_scales)
-        load_scale_rows(nc.sync, w1s_raw, w1_scales)
 
         xs_picked = keep.tile([P, PASSES, S], U8, name="xs_picked", align_bytes=64)
-        xw = [keep.tile([P, S], U32, name="xw%d" % o, align_bytes=64) for o in range(PASSES)]
+        xw = [keep.tile([P, S], U32, name="xw0", tag="after_xw0", align_bytes=64)]
         w2s = keep.tile([P, PASSES, H], U8, name="w2s", align_bytes=64)
         w1s = keep.tile([P, PASSES, H], U8, name="w1s", align_bytes=64)
         w2w = keep.tile([P, PASSES, 2 * H], U8, name="w2w", align_bytes=64)
@@ -94,21 +101,21 @@ def tile_picked_yleeca_log_p_kernel(
 
         for o in range(PASSES):
             nc.vector.tensor_copy(xs_picked[:, o, :], xs_all[:, o, :].indirect(offs_t[:]))
-        xw_second = keep.tile([P, T], U32, name="xw_second", tag="second", align_bytes=64)
-        nc.scalar.dma_start(out=xw_second[:].bitcast(I32), in_=x_words[1].rearrange("p n t -> p (n t)").bitcast(I32))
         for q in range(QUADS):
             nc.sync.dma_start(
                 out=xs[32 * q : 32 * q + 4, :, :].bitcast(I32), in_=xs_picked[ROW0 + 4 * q : ROW0 + 4 * q + 4, :, :].bitcast(I32)
             )
+        w1s_raw = keep.tile([P, PASSES, H], U8, name="w1s_raw", tag="after_xs", align_bytes=64)
+        nc.vector.memset(w1s_raw[:].bitcast(I32), 0)
+        load_scale_rows(nc.sync, w1s_raw, w1_scales)
         nc.vector.tensor_copy(xw[0][:], xw_first[:].indirect(offs_t[:]))
         deal_words(w2w, w2w_raw)
         deal_words(w1w, w1w_raw)
         deal_scales(w2s, w2s_raw)
-        deal_scales(w1s, w1s_raw)
+        xw.append(keep.tile([P, S], U32, name="xw1", tag="after_w2s", align_bytes=64))
         nc.vector.tensor_copy(xw[1][:], xw_second[:].indirect(offs_t[:]))
+        deal_scales(w1s, w1s_raw)
 
-        nc.sync.dma_start(out=w2w_raw[:, 0, 0 : 2 * N].bitcast(I32), in_=w3_words[0].bitcast(I32))
-        load_scale_rows(nc.sync, w2s_raw[:, 0:1, 0:N], w3_scales)
 
         ya_ps = [psum.tile([P, S], F32, name="ya_ps%d" % t, tag="ya%d" % t) for t in range(PACK)]
         kt_ps = [psum.tile([P, S], F32, name="kt_ps%d" % t, tag="kt%d" % t) for t in range(PACK)]
@@ -124,62 +131,70 @@ def tile_picked_yleeca_log_p_kernel(
                 stop=(o == PASSES - 1),
             )
 
-        for o in range(PASSES):
-            for t in range(PACK):
+        for t in range(PACK):
+            for o in range(PASSES):
                 product(ya_ps[t], w2w, w2s, t, o)
+            for o in range(PASSES):
                 product(kt_ps[t], w1w, w1s, t, o)
 
-        cohort = [keep.tile([P, S], F32, name="cohort%d" % t) for t in range(PACK)]
-        period = [keep.tile([P, S], F32, name="period%d" % t) for t in range(PACK)]
-        fetched = [keep.tile([P, S], F32, name="fetched%d" % t) for t in range(PACK)]
-        earlier = [keep.tile([P, S], F32, name="earlier%d" % t) for t in range(PACK)]
+        w3w = keep.tile([P, 2 * N], U8, name="w3w", tag="after_xw0", align_bytes=64)
+        w3s = keep.tile([P, 1, N], U8, name="w3s", tag="after_w2s", align_bytes=64)
+        nc.sync.dma_start(out=w3w[:].bitcast(I32), in_=w3_words[0].bitcast(I32))
+        nc.gpsimd.memset(w3s[:].bitcast(I32), 0)
+        load_scale_rows(nc.sync, w3s, w3_scales)
+
         lm = [keep.tile([P, S], F32, name="lm%d" % t) for t in range(PACK)]
         th = [keep.tile([P, S], F32, name="th%d" % t) for t in range(PACK)]
-        mx = [keep.tile([P, S], F32, name="mx%d" % t) for t in range(PACK)]
-        change = [keep.tile([P, S], F32, name="change%d" % t) for t in range(PACK)]
-        alive = keep.tile([P, PACK, S], F32, name="alive")
-        logq = keep.tile([P, PACK, S], F32, name="logq")
-
-        def fetch(dst, window, lst):
-            for c0 in range(0, S, HALF):
-                nc.vector.tensor_copy(dst[:, c0 : c0 + HALF], window[:].indirect(lst[:, c0 // 16 : (c0 + HALF) // 16]))
+        mx = [keep.tile([P, S], F32, name="mx%d" % t, tag="mx%d" % t) for t in range(PACK)]
+        alive = [keep.tile([P, S], F32, name="alive%d" % t) for t in range(PACK)]
 
         for t in range(PACK):
-            nc.scalar.activation(out=cohort[t][:], in_=ya_ps[t][:], func=ACT.Copy, scale=gx_t[:, t : t + 1])
-            nc.scalar.activation(out=period[t][:], in_=kt_ps[t][:], func=ACT.Copy, scale=unit_t[:, t : t + 1])
+            nc.scalar.activation(out=rows(cohort, t), in_=ya_ps[t][:], func=ACT.Copy, scale=gx_t[:, t : t + 1])
+            if t < PACK - ON_VECTOR:
+                nc.scalar.activation(out=rows(period, t), in_=kt_ps[t][:], func=ACT.Copy, scale=unit_t[:, t : t + 1])
         for t in range(PACK):
-            fetch(fetched[t], cohort[t], coh_t)
+            fetched = keep.tile([P, S], F32, name="fetched%d" % t, tag="after_xs", align_bytes=64)
+            nc.vector.tensor_copy(fetched[:], rows(cohort, t, S + SPARE).indirect(coh_t[:]))
             nc.vector.scalar_tensor_tensor(
-                out=lm[t][:], in0=kt_ps[t][:], scalar=bx_t[:, t : t + 1], in1=fetched[t][:], op0=ALU.mult, op1=ALU.add
+                out=lm[t][:], in0=kt_ps[t][:], scalar=bx_t[:, t : t + 1], in1=fetched[:], op0=ALU.mult, op1=ALU.add
             )
         for t in range(PACK):
             nc.scalar.activation(out=th[t][:], in_=lm[t][:], func=ACT.Tanh)
             nc.scalar.activation(out=mx[t][:], in_=th[t][:], func=ACT.Exp, scale=1.2)
-            nc.scalar.activation(out=alive[:, t, :], in_=mx[t][:], func=ACT.Exp, scale=-1.0)
+            nc.scalar.activation(out=alive[t][:], in_=mx[t][:], func=ACT.Exp, scale=-1.0)
+        for t in range(PACK - ON_VECTOR, PACK):
+            nc.vector.tensor_scalar(
+                out=rows(period, t), in0=kt_ps[t][:], scalar1=unit_t[:, t : t + 1], scalar2=None, op0=ALU.mult
+            )
+        earlier = keep.tile([P, PACK, S], F32, name="earlier", tag="after_xs", align_bytes=64)
         for t in range(PACK):
-            fetch(earlier[t], period[t], prv_t)
+            nc.vector.tensor_copy(earlier[:, t, :], rows(period, t, S + SPARE).indirect(prv_t[:]))
+
+        logq = keep.tile([P, PACK, S], F32, name="logq", tag="mx%d" % (PACK - 1))
+        level = keep.tile([P, PACK, S], F32, name="level")
+        for t in range(PACK):
+            nc.scalar.activation(out=logq[:, t, :], in_=alive[t][:], func=ACT.Ln, scale=-1.0, bias=1.05)
             nc.vector.scalar_tensor_tensor(
-                out=change[t][:], in0=kt_ps[t][:], scalar=unit_t[:, t : t + 1], in1=earlier[t][:], op0=ALU.mult, op1=ALU.subtract
+                out=level[:, t, :], in0=logq[:, t, :], scalar=unit_t[:, t : t + 1], in1=rows(period, t), op0=ALU.mult, op1=ALU.add
             )
 
         for i, (c0, n) in enumerate(PIECES):
             cols = slice(c0, c0 + n)
-            nc.scalar.activation(out=logq[:, :, cols], in_=alive[:, :, cols], func=ACT.Ln, scale=-1.0, bias=1.05)
-            hid = keep.tile([P, PACK, n], BF16, name="hid%d" % i, align_bytes=64)
-            for t in range(PACK):
-                nc.vector.scalar_tensor_tensor(
-                    out=hid[:, t, :], in0=logq[:, t, cols], scalar=unit_t[:, t : t + 1], in1=change[t][:, cols], op0=ALU.mult, op1=ALU.add
-                )
             woven = keep.tile([P, n, PACK], BF16, name="woven%d" % i, align_bytes=64)
-            nc.vector.tensor_copy(out=woven[:], in_=hid[:].rearrange("p t n -> p n t"))
+            nc.vector.tensor_tensor(
+                out=woven[:].rearrange("p (c e) t -> p c t e", e=2),
+                in0=level[:, :, cols].rearrange("p t (c e) -> p c t e", e=2),
+                in1=earlier[:, :, cols].rearrange("p t (c e) -> p c t e", e=2),
+                op=ALU.subtract,
+            )
             codes = keep.tile([P, n], U32, name="codes%d" % i, align_bytes=64)
             plane = keep.tile([P, n], U8, name="plane%d" % i, align_bytes=64)
             nc.vector.quantize_mx(out=codes[:].bitcast(FP8X4), scales=plane[:], in_=woven[:].rearrange("p n t -> p (n t)"))
             acc = psum.tile([P, n], F32, name="out_ps%d" % i, tag="ya%d" % i)
             nc.tensor.matmul_mx(
                 out=acc[:],
-                lhsT=w2w_raw[:, 0, 0 : 2 * N].bitcast(FP4X4),
-                lhsT_scale=w2s_raw[:, 0, 0:N],
+                lhsT=w3w[:].bitcast(FP4X4),
+                lhsT_scale=w3s[:, 0, :],
                 rhs=codes[:].bitcast(FP8X4),
                 rhs_scale=plane[:],
                 start=True,

@@ -22,7 +22,7 @@ PASSES = K // (P * PACK)
 QUADS = 4
 SPARE = 192
 ROW0 = P - 16
-ON_VECTOR = 1
+HALF = S // 2
 PIECES = ((0, 256), (256, 128), (384, 128))
 
 
@@ -44,16 +44,13 @@ def tile_picked_yleeca_log_p_kernel(
         offs_t = keep.tile([P, S // 16], U16, name="offs_t")
         coh_t = keep.tile([P, S // 16], U16, name="coh_t")
         prv_t = keep.tile([P, S // 16], U16, name="prv_t")
-        xs_all = keep.tile([P, PASSES, T], U8, name="xs_all", tag="after_xs", align_bytes=64)
+        xs_all = keep.tile([P, PASSES, T], U8, name="xs_all", tag="fetched0", align_bytes=64)
         xs = keep.tile([P, PASSES, S], U8, name="xs", align_bytes=64)
-        w2s_raw = keep.tile([P, PASSES, H], U8, name="w2s_raw", tag="after_w2s", align_bytes=64)
+        w2s_raw = keep.tile([P, PASSES, H], U8, name="w2s_raw", tag="xw1", align_bytes=64)
         nc.vector.memset(w2s_raw[:].bitcast(I32), 0)
         nc.vector.memset(xs_all[0:ROW0, :, :].bitcast(I32), 0)
         nc.vector.memset(xs[:].bitcast(I32), 0)
-        cohort = keep.tile([P, PACK * S + SPARE], F32, name="cohort")
-        period = keep.tile([P, PACK * S + SPARE], F32, name="period")
-        nc.vector.memset(cohort[:, PACK * S :], 0.0)
-        nc.vector.memset(period[:, PACK * S :], 0.0)
+        cohort = keep.tile([P, PACK * S], F32, name="cohort")
 
         def rows(tile, t, width=S):
             c0 = (PACK - 1 - t) * S
@@ -81,7 +78,7 @@ def tile_picked_yleeca_log_p_kernel(
         load_scale_rows(nc.scalar, w2s_raw, w2_scales)
 
         xs_picked = keep.tile([P, PASSES, S], U8, name="xs_picked", align_bytes=64)
-        xw = [keep.tile([P, S], U32, name="xw0", tag="after_xw0", align_bytes=64)]
+        xw = [keep.tile([P, S], U32, name="xw0", tag="xw0", align_bytes=64)]
         w2s = keep.tile([P, PASSES, H], U8, name="w2s", align_bytes=64)
         w1s = keep.tile([P, PASSES, H], U8, name="w1s", align_bytes=64)
         w2w = keep.tile([P, PASSES, 2 * H], U8, name="w2w", align_bytes=64)
@@ -105,14 +102,14 @@ def tile_picked_yleeca_log_p_kernel(
             nc.sync.dma_start(
                 out=xs[32 * q : 32 * q + 4, :, :].bitcast(I32), in_=xs_picked[ROW0 + 4 * q : ROW0 + 4 * q + 4, :, :].bitcast(I32)
             )
-        w1s_raw = keep.tile([P, PASSES, H], U8, name="w1s_raw", tag="after_xs", align_bytes=64)
+        w1s_raw = keep.tile([P, PASSES, H], U8, name="w1s_raw", tag="fetched0", align_bytes=64)
         nc.vector.memset(w1s_raw[:].bitcast(I32), 0)
-        load_scale_rows(nc.sync, w1s_raw, w1_scales)
+        load_scale_rows(nc.scalar, w1s_raw, w1_scales)
         nc.vector.tensor_copy(xw[0][:], xw_first[:].indirect(offs_t[:]))
         deal_words(w2w, w2w_raw)
         deal_words(w1w, w1w_raw)
         deal_scales(w2s, w2s_raw)
-        xw.append(keep.tile([P, S], U32, name="xw1", tag="after_w2s", align_bytes=64))
+        xw.append(keep.tile([P, S], U32, name="xw1", tag="xw1", align_bytes=64))
         nc.vector.tensor_copy(xw[1][:], xw_second[:].indirect(offs_t[:]))
         deal_scales(w1s, w1s_raw)
 
@@ -120,25 +117,28 @@ def tile_picked_yleeca_log_p_kernel(
         ya_ps = [psum.tile([P, S], F32, name="ya_ps%d" % t, tag="ya%d" % t) for t in range(PACK)]
         kt_ps = [psum.tile([P, S], F32, name="kt_ps%d" % t, tag="kt%d" % t) for t in range(PACK)]
 
-        def product(acc, words, scales, t, o):
+        def product(acc, words, scales, t, order):
+          for o in order:
             nc.tensor.matmul_mx(
                 out=acc[:],
                 lhsT=words[:, o, 2 * P * t : 2 * P * (t + 1)].bitcast(FP4X4),
                 lhsT_scale=scales[:, o, P * t : P * (t + 1)],
                 rhs=xw[o][:].bitcast(FP8X4),
                 rhs_scale=xs[:, o, :],
-                start=(o == 0),
-                stop=(o == PASSES - 1),
+                start=(o == order[0]),
+                stop=(o == order[-1]),
             )
 
-        for t in range(PACK):
-            for o in range(PASSES):
-                product(ya_ps[t], w2w, w2s, t, o)
-            for o in range(PASSES):
-                product(kt_ps[t], w1w, w1s, t, o)
+        product(ya_ps[0], w2w, w2s, 0, (0, 1))
+        for t in range(1, PACK - 1):
+            product(ya_ps[t], w2w, w2s, t, (1, 0))
+        product(kt_ps[0], w1w, w1s, 0, (1, 0))
+        product(ya_ps[PACK - 1], w2w, w2s, PACK - 1, (1, 0))
+        for t in range(1, PACK):
+            product(kt_ps[t], w1w, w1s, t, (1, 0))
 
-        w3w = keep.tile([P, 2 * N], U8, name="w3w", tag="after_xw0", align_bytes=64)
-        w3s = keep.tile([P, 1, N], U8, name="w3s", tag="after_w2s", align_bytes=64)
+        w3w = keep.tile([P, 2 * N], U8, name="w3w", tag="xw0", align_bytes=64)
+        w3s = keep.tile([P, 1, N], U8, name="w3s", tag="xw1", align_bytes=64)
         nc.sync.dma_start(out=w3w[:].bitcast(I32), in_=w3_words[0].bitcast(I32))
         nc.gpsimd.memset(w3s[:].bitcast(I32), 0)
         load_scale_rows(nc.sync, w3s, w3_scales)
@@ -146,15 +146,16 @@ def tile_picked_yleeca_log_p_kernel(
         lm = [keep.tile([P, S], F32, name="lm%d" % t) for t in range(PACK)]
         th = [keep.tile([P, S], F32, name="th%d" % t) for t in range(PACK)]
         mx = [keep.tile([P, S], F32, name="mx%d" % t, tag="mx%d" % t) for t in range(PACK)]
-        alive = [keep.tile([P, S], F32, name="alive%d" % t) for t in range(PACK)]
+        alive = [keep.tile([P, S], F32, name="alive%d" % t, tag="alive%d" % t) for t in range(PACK)]
 
         for t in range(PACK):
             nc.scalar.activation(out=rows(cohort, t), in_=ya_ps[t][:], func=ACT.Copy, scale=gx_t[:, t : t + 1])
-            if t < PACK - ON_VECTOR:
-                nc.scalar.activation(out=rows(period, t), in_=kt_ps[t][:], func=ACT.Copy, scale=unit_t[:, t : t + 1])
-        for t in range(PACK):
-            fetched = keep.tile([P, S], F32, name="fetched%d" % t, tag="after_xs", align_bytes=64)
-            nc.vector.tensor_copy(fetched[:], rows(cohort, t, S + SPARE).indirect(coh_t[:]))
+            fetched = keep.tile([P, S], F32, name="fetched%d" % t, tag="fetched%d" % int(t == 2), align_bytes=64)
+            if t == 0:
+                nc.vector.tensor_copy(fetched[:, 0:HALF], rows(cohort, t).indirect(coh_t[:, 0 : HALF // 16]))
+                nc.scalar.activation(out=fetched[:, HALF:S], in_=rows(cohort, t).indirect(coh_t[:, HALF // 16 :]), func=ACT.Copy)
+            else:
+                nc.vector.tensor_copy(fetched[:], rows(cohort, t, S + SPARE).indirect(coh_t[:]))
             nc.vector.scalar_tensor_tensor(
                 out=lm[t][:], in0=kt_ps[t][:], scalar=bx_t[:, t : t + 1], in1=fetched[:], op0=ALU.mult, op1=ALU.add
             )
@@ -162,29 +163,40 @@ def tile_picked_yleeca_log_p_kernel(
             nc.scalar.activation(out=th[t][:], in_=lm[t][:], func=ACT.Tanh)
             nc.scalar.activation(out=mx[t][:], in_=th[t][:], func=ACT.Exp, scale=1.2)
             nc.scalar.activation(out=alive[t][:], in_=mx[t][:], func=ACT.Exp, scale=-1.0)
-        for t in range(PACK - ON_VECTOR, PACK):
-            nc.vector.tensor_scalar(
-                out=rows(period, t), in0=kt_ps[t][:], scalar1=unit_t[:, t : t + 1], scalar2=None, op0=ALU.mult
-            )
-        earlier = keep.tile([P, PACK, S], F32, name="earlier", tag="after_xs", align_bytes=64)
+        period_all = keep.tile([P, PACK, S], F32, name="period_all", tag="fetched0", align_bytes=64)
+        period = [period_all[:, t, :] for t in range(PACK)]
         for t in range(PACK):
-            nc.vector.tensor_copy(earlier[:, t, :], rows(period, t, S + SPARE).indirect(prv_t[:]))
+            nc.vector.tensor_scalar(
+                out=period[t], in0=kt_ps[t][:], scalar1=unit_t[:, t : t + 1], scalar2=None, op0=ALU.mult
+            )
+        earlier_low = keep.tile([P, PACK, HALF], F32, name="earlier_low")
+        for t in range(PACK):
+            nc.vector.tensor_copy(earlier_low[:, t, :], period[t].indirect(prv_t[:, 0 : HALF // 16]))
 
         logq = keep.tile([P, PACK, S], F32, name="logq", tag="mx%d" % (PACK - 1))
         level = keep.tile([P, PACK, S], F32, name="level")
         for t in range(PACK):
             nc.scalar.activation(out=logq[:, t, :], in_=alive[t][:], func=ACT.Ln, scale=-1.0, bias=1.05)
             nc.vector.scalar_tensor_tensor(
-                out=level[:, t, :], in0=logq[:, t, :], scalar=unit_t[:, t : t + 1], in1=rows(period, t), op0=ALU.mult, op1=ALU.add
+                out=level[:, t, :], in0=logq[:, t, :], scalar=unit_t[:, t : t + 1], in1=period[t], op0=ALU.mult, op1=ALU.add
             )
+        earlier_high = keep.tile([P, PACK, HALF], F32, name="earlier_high", tag="alive%d" % (PACK - 1))
+        for c0, n in PIECES[1:]:
+            for t in range(PACK):
+                nc.scalar.activation(
+                    out=earlier_high[:, t, c0 - HALF : c0 - HALF + n],
+                    in_=period[t].indirect(prv_t[:, c0 // 16 : (c0 + n) // 16]),
+                    func=ACT.Copy,
+                )
 
         for i, (c0, n) in enumerate(PIECES):
             cols = slice(c0, c0 + n)
+            earlier = earlier_low[:, :, cols] if c0 < HALF else earlier_high[:, :, c0 - HALF : c0 - HALF + n]
             woven = keep.tile([P, n, PACK], BF16, name="woven%d" % i, align_bytes=64)
             nc.vector.tensor_tensor(
                 out=woven[:].rearrange("p (c e) t -> p c t e", e=2),
                 in0=level[:, :, cols].rearrange("p t (c e) -> p c t e", e=2),
-                in1=earlier[:, :, cols].rearrange("p t (c e) -> p c t e", e=2),
+                in1=earlier.rearrange("p t (c e) -> p c t e", e=2),
                 op=ALU.subtract,
             )
             codes = keep.tile([P, n], U32, name="codes%d" % i, align_bytes=64)

@@ -44,17 +44,20 @@ def tile_picked_yleeca_log_p_kernel(
         offs_t = keep.tile([P, S // 16], U16, name="offs_t")
         coh_t = keep.tile([P, S // 16], U16, name="coh_t")
         prv_t = keep.tile([P, S // 16], U16, name="prv_t")
-        xs_all = keep.tile([P, PASSES, T], U8, name="xs_all", tag="fetched0", align_bytes=64)
+        xs_all = keep.tile([P, PASSES, T], U8, name="xs_all", align_bytes=64)
         xs = keep.tile([P, PASSES, S], U8, name="xs", align_bytes=64)
         w2s_raw = keep.tile([P, PASSES, H], U8, name="w2s_raw", tag="xw1", align_bytes=64)
+        w1s_raw = keep.tile([P, PASSES, H], U8, name="w1s_raw", tag="fetched0", align_bytes=64)
         nc.vector.memset(w2s_raw[:].bitcast(I32), 0)
         nc.vector.memset(xs_all[0:ROW0, :, :].bitcast(I32), 0)
         nc.vector.memset(xs[:].bitcast(I32), 0)
+        nc.vector.memset(w1s_raw[:].bitcast(I32), 0)
+
         cohort = keep.tile([P, PACK * S], F32, name="cohort")
 
-        def rows(tile, t, width=S):
-            c0 = (PACK - 1 - t) * S
-            return tile[:, c0 : c0 + width]
+        def cohort_slab(t, width=S):
+            first = (PACK - 1 - t) * S
+            return cohort[:, first : first + width]
 
         nc.sync.dma_start(offs_t[:], offs)
         nc.scalar.dma_start(out=xs_all[ROW0:P, :, :].bitcast(I32), in_=x_scales.rearrange("o q c -> q o c").bitcast(I32))
@@ -73,9 +76,10 @@ def tile_picked_yleeca_log_p_kernel(
         nc.gpsimd.dma_start(out=w2w_raw[:].bitcast(I32), in_=w2_words.rearrange("o p c -> p o c").bitcast(I32))
         nc.gpsimd.dma_start(out=xw_second[:].bitcast(I32), in_=x_words[1].rearrange("p n t -> p (n t)").bitcast(I32))
         nc.gpsimd.dma_start(out=w1w_raw[:].bitcast(I32), in_=w1_words.rearrange("o p c -> p o c").bitcast(I32))
-        nc.gpsimd.dma_start(out=unit_t[:], in_=unit.rearrange("(p t) one -> p (t one)", t=PACK))
         nc.gpsimd.dma_start(out=bx_t[:], in_=bx.rearrange("(p t) one -> p (t one)", t=PACK))
+        nc.gpsimd.dma_start(out=unit_t[:], in_=unit.rearrange("(p t) one -> p (t one)", t=PACK))
         load_scale_rows(nc.scalar, w2s_raw, w2_scales)
+        load_scale_rows(nc.scalar, w1s_raw, w1_scales)
 
         xs_picked = keep.tile([P, PASSES, S], U8, name="xs_picked", align_bytes=64)
         xw = [keep.tile([P, S], U32, name="xw0", tag="xw0", align_bytes=64)]
@@ -102,9 +106,6 @@ def tile_picked_yleeca_log_p_kernel(
             nc.sync.dma_start(
                 out=xs[32 * q : 32 * q + 4, :, :].bitcast(I32), in_=xs_picked[ROW0 + 4 * q : ROW0 + 4 * q + 4, :, :].bitcast(I32)
             )
-        w1s_raw = keep.tile([P, PASSES, H], U8, name="w1s_raw", tag="fetched0", align_bytes=64)
-        nc.vector.memset(w1s_raw[:].bitcast(I32), 0)
-        load_scale_rows(nc.scalar, w1s_raw, w1_scales)
         nc.vector.tensor_copy(xw[0][:], xw_first[:].indirect(offs_t[:]))
         deal_words(w2w, w2w_raw)
         deal_words(w1w, w1w_raw)
@@ -113,27 +114,26 @@ def tile_picked_yleeca_log_p_kernel(
         nc.vector.tensor_copy(xw[1][:], xw_second[:].indirect(offs_t[:]))
         deal_scales(w1s, w1s_raw)
 
-
         ya_ps = [psum.tile([P, S], F32, name="ya_ps%d" % t, tag="ya%d" % t) for t in range(PACK)]
         kt_ps = [psum.tile([P, S], F32, name="kt_ps%d" % t, tag="kt%d" % t) for t in range(PACK)]
 
         def product(acc, words, scales, t, order):
-          for o in order:
-            nc.tensor.matmul_mx(
-                out=acc[:],
-                lhsT=words[:, o, 2 * P * t : 2 * P * (t + 1)].bitcast(FP4X4),
-                lhsT_scale=scales[:, o, P * t : P * (t + 1)],
-                rhs=xw[o][:].bitcast(FP8X4),
-                rhs_scale=xs[:, o, :],
-                start=(o == order[0]),
-                stop=(o == order[-1]),
-            )
+            for o in order:
+                nc.tensor.matmul_mx(
+                    out=acc[:],
+                    lhsT=words[:, o, 2 * P * t : 2 * P * (t + 1)].bitcast(FP4X4),
+                    lhsT_scale=scales[:, o, P * t : P * (t + 1)],
+                    rhs=xw[o][:].bitcast(FP8X4),
+                    rhs_scale=xs[:, o, :],
+                    start=(o == order[0]),
+                    stop=(o == order[-1]),
+                )
 
         product(ya_ps[0], w2w, w2s, 0, (0, 1))
-        for t in range(1, PACK - 1):
-            product(ya_ps[t], w2w, w2s, t, (1, 0))
+        product(ya_ps[1], w2w, w2s, 1, (1, 0))
         product(kt_ps[0], w1w, w1s, 0, (1, 0))
-        product(ya_ps[PACK - 1], w2w, w2s, PACK - 1, (1, 0))
+        for t in range(2, PACK):
+            product(ya_ps[t], w2w, w2s, t, (1, 0))
         for t in range(1, PACK):
             product(kt_ps[t], w1w, w1s, t, (1, 0))
 
@@ -149,20 +149,22 @@ def tile_picked_yleeca_log_p_kernel(
         alive = [keep.tile([P, S], F32, name="alive%d" % t, tag="alive%d" % t) for t in range(PACK)]
 
         for t in range(PACK):
-            nc.scalar.activation(out=rows(cohort, t), in_=ya_ps[t][:], func=ACT.Copy, scale=gx_t[:, t : t + 1])
+            nc.scalar.activation(out=cohort_slab(t), in_=ya_ps[t][:], func=ACT.Copy, scale=gx_t[:, t : t + 1])
             fetched = keep.tile([P, S], F32, name="fetched%d" % t, tag="fetched%d" % int(t == 2), align_bytes=64)
             if t == 0:
-                nc.vector.tensor_copy(fetched[:, 0:HALF], rows(cohort, t).indirect(coh_t[:, 0 : HALF // 16]))
-                nc.scalar.activation(out=fetched[:, HALF:S], in_=rows(cohort, t).indirect(coh_t[:, HALF // 16 :]), func=ACT.Copy)
+                nc.vector.tensor_copy(fetched[:, 0:HALF], cohort_slab(t).indirect(coh_t[:, 0 : HALF // 16]))
+                nc.scalar.activation(out=fetched[:, HALF:S], in_=cohort_slab(t).indirect(coh_t[:, HALF // 16 :]), func=ACT.Copy)
             else:
-                nc.vector.tensor_copy(fetched[:], rows(cohort, t, S + SPARE).indirect(coh_t[:]))
+                nc.vector.tensor_copy(fetched[:], cohort_slab(t, S + SPARE).indirect(coh_t[:]))
             nc.vector.scalar_tensor_tensor(
                 out=lm[t][:], in0=kt_ps[t][:], scalar=bx_t[:, t : t + 1], in1=fetched[:], op0=ALU.mult, op1=ALU.add
             )
+
         for t in range(PACK):
             nc.scalar.activation(out=th[t][:], in_=lm[t][:], func=ACT.Tanh)
             nc.scalar.activation(out=mx[t][:], in_=th[t][:], func=ACT.Exp, scale=1.2)
             nc.scalar.activation(out=alive[t][:], in_=mx[t][:], func=ACT.Exp, scale=-1.0)
+
         period_all = keep.tile([P, PACK, S], F32, name="period_all", tag="fetched0", align_bytes=64)
         period = [period_all[:, t, :] for t in range(PACK)]
         for t in range(PACK):

from contextlib import ExitStack

import concourse.mybir as mybir

K, T, S, N, H = 1024, 2048, 512, 128, 512
FLOPS = 2 * (2 * K * H * S + H * N * S)

F32 = mybir.dt.float32
BF16 = mybir.dt.bfloat16
I32 = mybir.dt.int32
U32 = mybir.dt.uint32
U16 = mybir.dt.uint16
U8 = mybir.dt.uint8
FP8X4 = mybir.dt.float8_e4m3fn_x4
FP4X4 = mybir.dt.float4_e2m1fn_x4
ACT = mybir.ActivationFunctionType
ALU = mybir.AluOpType

P = 128
PACK = 4
PASSES = K // (P * PACK)
QUADS = 4
SPARE = 192
ROW0 = P - 16
HALF = S // 2
PIECES = ((0, 256), (256, 128), (384, 128))


def tile_picked_yleeca_log_p_kernel(
    tc, x_words, x_scales, w1_words, w1_scales, w2_words, w2_scales, bx, gx, unit, w3_words, w3_scales, offs, prv, coh, out
):
    nc = tc.nc
    with ExitStack() as ctx:
        keep = ctx.enter_context(tc.tile_pool(name="keep", bufs=1))
        psum = ctx.enter_context(tc.psum_pool(name="psum", bufs=1))

        def load_scale_rows(queue, plane, scales):
            for q in range(QUADS):
                queue.dma_start(
                    out=plane[32 * q : 32 * q + 4, :, :].bitcast(I32),
                    in_=scales[:, 4 * q : 4 * q + 4, :].rearrange("o r c -> r o c").bitcast(I32),
                )

        offs_t = keep.tile([P, S // 16], U16, name="offs_t")
        coh_t = keep.tile([P, S // 16], U16, name="coh_t")
        prv_t = keep.tile([P, S // 16], U16, name="prv_t")
        xs_all = keep.tile([P, PASSES, T], U8, name="xs_all", align_bytes=64)
        xs = keep.tile([P, PASSES, S], U8, name="xs", align_bytes=64)
        w2s_raw = keep.tile([P, PASSES, H], U8, name="w2s_raw", tag="xw1", align_bytes=64)
        w1s_raw = keep.tile([P, PASSES, H], U8, name="w1s_raw", tag="fetched0", align_bytes=64)
        nc.vector.memset(w2s_raw[:].bitcast(I32), 0)
        nc.vector.memset(xs_all[0:ROW0, :, :].bitcast(I32), 0)
        nc.vector.memset(xs[:].bitcast(I32), 0)
        nc.vector.memset(w1s_raw[:].bitcast(I32), 0)

        cohort = keep.tile([P, PACK * S], F32, name="cohort")

        def cohort_slab(t, width=S):
            first = (PACK - 1 - t) * S
            return cohort[:, first : first + width]

        nc.sync.dma_start(offs_t[:], offs)
        nc.scalar.dma_start(out=xs_all[ROW0:P, :, :].bitcast(I32), in_=x_scales.rearrange("o q c -> q o c").bitcast(I32))

        xw_first = keep.tile([P, T], U32, name="xw_first", align_bytes=64)
        xw_second = keep.tile([P, T], U32, name="xw_second", align_bytes=64)
        w2w_raw = keep.tile([P, PASSES, 2 * H], U8, name="w2w_raw", align_bytes=64)
        w1w_raw = keep.tile([P, PASSES, 2 * H], U8, name="w1w_raw", align_bytes=64)
        gx_t = keep.tile([P, PACK], F32, name="gx_t")
        bx_t = keep.tile([P, PACK], F32, name="bx_t")
        unit_t = keep.tile([P, PACK], F32, name="unit_t")
        nc.sync.dma_start(out=xw_first[:].bitcast(I32), in_=x_words[0].rearrange("p n t -> p (n t)").bitcast(I32))
        nc.sync.dma_start(coh_t[:], coh)
        nc.sync.dma_start(prv_t[:], prv)
        nc.sync.dma_start(out=gx_t[:], in_=gx.rearrange("(p t) one -> p (t one)", t=PACK))
        nc.gpsimd.dma_start(out=w2w_raw[:].bitcast(I32), in_=w2_words.rearrange("o p c -> p o c").bitcast(I32))
        nc.gpsimd.dma_start(out=xw_second[:].bitcast(I32), in_=x_words[1].rearrange("p n t -> p (n t)").bitcast(I32))
        nc.gpsimd.dma_start(out=w1w_raw[:].bitcast(I32), in_=w1_words.rearrange("o p c -> p o c").bitcast(I32))
        nc.gpsimd.dma_start(out=bx_t[:], in_=bx.rearrange("(p t) one -> p (t one)", t=PACK))
        nc.gpsimd.dma_start(out=unit_t[:], in_=unit.rearrange("(p t) one -> p (t one)", t=PACK))
        load_scale_rows(nc.scalar, w2s_raw, w2_scales)
        load_scale_rows(nc.scalar, w1s_raw, w1_scales)

        xs_picked = keep.tile([P, PASSES, S], U8, name="xs_picked", align_bytes=64)
        xw = [keep.tile([P, S], U32, name="xw0", tag="xw0", align_bytes=64)]
        w2s = keep.tile([P, PASSES, H], U8, name="w2s", align_bytes=64)
        w1s = keep.tile([P, PASSES, H], U8, name="w1s", align_bytes=64)
        w2w = keep.tile([P, PASSES, 2 * H], U8, name="w2w", align_bytes=64)
        w1w = keep.tile([P, PASSES, 2 * H], U8, name="w1w", align_bytes=64)

        def deal_scales(dealt, raw):
            nc.vector.tensor_copy(
                out=dealt[:].rearrange("p o (t m) -> p o t m", t=PACK),
                in_=raw[:].rearrange("p o (m t) -> p o t m", t=PACK),
            )

        def deal_words(dealt, raw):
            nc.scalar.copy(
                out=dealt[:].bitcast(U16).rearrange("p o (t m) -> p o t m", t=PACK),
                in_=raw[:].bitcast(U16).rearrange("p o (m t) -> p o t m", t=PACK),
            )

        for o in range(PASSES):
            nc.vector.tensor_copy(xs_picked[:, o, :], xs_all[:, o, :].indirect(offs_t[:]))
        for q in range(QUADS):
            nc.sync.dma_start(
                out=xs[32 * q : 32 * q + 4, :, :].bitcast(I32), in_=xs_picked[ROW0 + 4 * q : ROW0 + 4 * q + 4, :, :].bitcast(I32)
            )
        nc.vector.tensor_copy(xw[0][:], xw_first[:].indirect(offs_t[:]))
        deal_words(w2w, w2w_raw)
        deal_words(w1w, w1w_raw)
        deal_scales(w2s, w2s_raw)
        xw.append(keep.tile([P, S], U32, name="xw1", tag="xw1", align_bytes=64))
        nc.vector.tensor_copy(xw[1][:], xw_second[:].indirect(offs_t[:]))
        deal_scales(w1s, w1s_raw)

        ya_ps = [psum.tile([P, S], F32, name="ya_ps%d" % t, tag="ya%d" % t) for t in range(PACK)]
        kt_ps = [psum.tile([P, S], F32, name="kt_ps%d" % t, tag="kt%d" % t) for t in range(PACK)]

        def product(acc, words, scales, t, order):
            for o in order:
                nc.tensor.matmul_mx(
                    out=acc[:],
                    lhsT=words[:, o, 2 * P * t : 2 * P * (t + 1)].bitcast(FP4X4),
                    lhsT_scale=scales[:, o, P * t : P * (t + 1)],
                    rhs=xw[o][:].bitcast(FP8X4),
                    rhs_scale=xs[:, o, :],
                    start=(o == order[0]),
                    stop=(o == order[-1]),
                )

        product(ya_ps[0], w2w, w2s, 0, (0, 1))
        product(ya_ps[1], w2w, w2s, 1, (1, 0))
        product(kt_ps[0], w1w, w1s, 0, (1, 0))
        for t in range(2, PACK):
            product(ya_ps[t], w2w, w2s, t, (1, 0))
        for t in range(1, PACK):
            product(kt_ps[t], w1w, w1s, t, (1, 0))

        w3w = keep.tile([P, 2 * N], U8, name="w3w", tag="xw0", align_bytes=64)
        w3s = keep.tile([P, 1, N], U8, name="w3s", tag="xw1", align_bytes=64)
        nc.sync.dma_start(out=w3w[:].bitcast(I32), in_=w3_words[0].bitcast(I32))
        nc.gpsimd.memset(w3s[:].bitcast(I32), 0)
        load_scale_rows(nc.sync, w3s, w3_scales)

        lm = [keep.tile([P, S], F32, name="lm%d" % t) for t in range(PACK)]
        th = [keep.tile([P, S], F32, name="th%d" % t) for t in range(PACK)]
        mx = [keep.tile([P, S], F32, name="mx%d" % t, tag="mx%d" % t) for t in range(PACK)]
        alive = [keep.tile([P, S], F32, name="alive%d" % t, tag="alive%d" % t) for t in range(PACK)]

        for t in range(PACK):
            nc.scalar.activation(out=cohort_slab(t), in_=ya_ps[t][:], func=ACT.Copy, scale=gx_t[:, t : t + 1])
            fetched = keep.tile([P, S], F32, name="fetched%d" % t, tag="fetched%d" % int(t == 2), align_bytes=64)
            if t == 0:
                nc.vector.tensor_copy(fetched[:, 0:HALF], cohort_slab(t).indirect(coh_t[:, 0 : HALF // 16]))
                nc.scalar.activation(out=fetched[:, HALF:S], in_=cohort_slab(t).indirect(coh_t[:, HALF // 16 :]), func=ACT.Copy)
            else:
                nc.vector.tensor_copy(fetched[:], cohort_slab(t, S + SPARE).indirect(coh_t[:]))
            nc.vector.scalar_tensor_tensor(
                out=lm[t][:], in0=kt_ps[t][:], scalar=bx_t[:, t : t + 1], in1=fetched[:], op0=ALU.mult, op1=ALU.add
            )

        for t in range(PACK):
            nc.scalar.activation(out=th[t][:], in_=lm[t][:], func=ACT.Tanh)
            nc.scalar.activation(out=mx[t][:], in_=th[t][:], func=ACT.Exp, scale=1.2)
            nc.scalar.activation(out=alive[t][:], in_=mx[t][:], func=ACT.Exp, scale=-1.0)

        period_all = keep.tile([P, PACK, S], F32, name="period_all", tag="fetched0", align_bytes=64)
        period = [period_all[:, t, :] for t in range(PACK)]
        for t in range(PACK):
            nc.vector.tensor_scalar(
                out=period[t], in0=kt_ps[t][:], scalar1=unit_t[:, t : t + 1], scalar2=None, op0=ALU.mult
            )
        earlier_low = keep.tile([P, PACK, HALF], F32, name="earlier_low")
        for t in range(PACK):
            nc.vector.tensor_copy(earlier_low[:, t, :], period[t].indirect(prv_t[:, 0 : HALF // 16]))

        logq = keep.tile([P, PACK, S], F32, name="logq", tag="mx%d" % (PACK - 1))
        level = keep.tile([P, PACK, S], F32, name="level")
        for t in range(PACK):
            nc.scalar.activation(out=logq[:, t, :], in_=alive[t][:], func=ACT.Ln, scale=-1.0, bias=1.05)
            nc.vector.scalar_tensor_tensor(
                out=level[:, t, :], in0=logq[:, t, :], scalar=unit_t[:, t : t + 1], in1=period[t], op0=ALU.mult, op1=ALU.add
            )
        earlier_high = keep.tile([P, PACK, HALF], F32, name="earlier_high", tag="alive%d" % (PACK - 1))
        for c0, n in PIECES[1:]:
            for t in range(PACK):
                nc.scalar.activation(
                    out=earlier_high[:, t, c0 - HALF : c0 - HALF + n],
                    in_=period[t].indirect(prv_t[:, c0 // 16 : (c0 + n) // 16]),
                    func=ACT.Copy,
                )

        for i, (c0, n) in enumerate(PIECES):
            cols = slice(c0, c0 + n)
            earlier = earlier_low[:, :, cols] if c0 < HALF else earlier_high[:, :, c0 - HALF : c0 - HALF + n]
            woven = keep.tile([P, n, PACK], BF16, name="woven%d" % i, align_bytes=64)
            nc.vector.tensor_tensor(
                out=woven[:].rearrange("p (c e) t -> p c t e", e=2),
                in0=level[:, :, cols].rearrange("p t (c e) -> p c t e", e=2),
                in1=earlier.rearrange("p t (c e) -> p c t e", e=2),
                op=ALU.subtract,
            )
            codes = keep.tile([P, n], U32, name="codes%d" % i, align_bytes=64)
            plane = keep.tile([P, n], U8, name="plane%d" % i, align_bytes=64)
            nc.vector.quantize_mx(out=codes[:].bitcast(FP8X4), scales=plane[:], in_=woven[:].rearrange("p n t -> p (n t)"))
            acc = psum.tile([P, n], F32, name="out_ps%d" % i, tag="ya%d" % i)
            nc.tensor.matmul_mx(
                out=acc[:],
                lhsT=w3w[:].bitcast(FP4X4),
                lhsT_scale=w3s[:, 0, :],
                rhs=codes[:].bitcast(FP8X4),
                rhs_scale=plane[:],
                start=True,
                stop=True,
            )
            res = keep.tile([P, n], F32, name="res%d" % i)
            nc.scalar.copy(out=res[:], in_=acc[:])
            nc.sync.dma_start(out=out[:, cols], in_=res[:])
